import numpy as np
import ml_dtypes


def mxq(x, axis, fmt="e4m3"):
    dtype, down = {"e4m3": (ml_dtypes.float8_e4m3fn, 7), "e5m2": (ml_dtypes.float8_e5m2, 14)}[fmt]
    v = np.moveaxis(np.asarray(x, np.float32).astype(ml_dtypes.bfloat16).astype(np.float64), axis, -1)
    blocks = v.reshape(v.shape[:-1] + (-1, 32))
    amax = np.abs(blocks).max(-1, keepdims=True)
    byte = np.maximum(np.where(amax > 0, np.frexp(amax)[1] - 1 + 127, 0) - down, 1)
    scale = np.exp2(byte - 127.0)
    codes = (blocks / scale).astype(np.float32).astype(dtype).astype(np.float64)
    return np.moveaxis((codes * scale).reshape(v.shape), -1, axis)


WIDE = False


def mx_kscale(k):
    if not WIDE:
        return np.ones(k)
    levels = np.array([10, -10, 5, -5, 0])
    if k % 512:
        return np.exp2(np.random.permutation(np.resize(levels, k // 32))).repeat(32)
    a = np.empty((k // 512, 16))
    for p in range(k // 512):
        a[p, :8] = np.random.permutation(np.resize(levels, 8))
        for g in range(8):
            far = levels[np.abs(levels - a[p, g]) >= 10]
            a[p, g + 8] = far[np.random.randint(len(far))]
    return np.exp2(a.ravel()).repeat(32)


def f64(x):
    return np.asarray(x).astype(np.float64)


def striped(idx):
    return np.tile(idx.reshape(-1, 16).T, (8, 1)).astype(np.uint16)


def unstriped(offs):
    return offs[:16].T.reshape(-1).astype(np.int64)


def striped8(idx):
    return np.concatenate([x.reshape(-1, 16).T for x in idx]).astype(np.uint16)


def runs(offs, k):
    lists = np.stack([offs[16 * r : 16 * r + 16].T.reshape(-1) for r in range(8)]).astype(np.int64)
    return lists[np.arange(k) % 512 // 64]


def pack_weight(w):
    k, n = w.shape
    w = f64(np.asarray(w, np.float32).astype(ml_dtypes.bfloat16)).reshape(k // 32, 32, n)
    amax = np.abs(w).max(1)
    byte = np.clip(np.where(amax > 0, np.frexp(amax)[1] - 1 + 127 - 7, 1), 1, 254)
    scaled = (w * np.exp2(127.0 - byte)[:, None, :]).reshape(k, n).astype(np.float32)
    words = np.ascontiguousarray(scaled.reshape(k // 512, 128, 4, n).transpose(0, 1, 3, 2)).astype(ml_dtypes.float8_e4m3fn).view(np.uint8)
    return words, np.ascontiguousarray(byte.astype(np.uint8).reshape(k // 512, 16, n))


def unpack_weight(words, scales):
    g, p, n, _ = words.shape
    vals = np.ascontiguousarray(words).view(ml_dtypes.float8_e4m3fn).astype(np.float64) * np.repeat(np.exp2(scales.astype(np.float64) - 127.0), 8, axis=1)[..., None]
    return vals.transpose(0, 1, 3, 2).reshape(g * 512, n)


E2M1 = np.array([0.0, 0.5, 1.0, 1.5, 2.0, 3.0, 4.0, 6.0, -0.0, -0.5, -1.0, -1.5, -2.0, -3.0, -4.0, -6.0])


def pack_fp4(w):
    k, n = w.shape
    w = f64(np.asarray(w, np.float32).astype(ml_dtypes.bfloat16)).reshape(k // 32, 32, n)
    amax = np.abs(w).max(1)
    mant, ex = np.frexp(amax / 6.0)
    byte = np.clip(np.where(amax > 0, np.where(mant > 0.5, ex, ex - 1) + 127, 1), 1, 254)
    scaled = (w * np.exp2(127.0 - byte)[:, None, :]).reshape(k, n).astype(np.float32)
    c = np.ascontiguousarray(scaled.reshape(k // 512, 128, 4, n).transpose(0, 1, 3, 2)).astype(ml_dtypes.float4_e2m1fn).view(np.uint8) & 0xF
    words = (c[..., 0::2] | (c[..., 1::2] << 4)).reshape(k // 512, 128, 2 * n)
    return np.ascontiguousarray(words), np.ascontiguousarray(byte.astype(np.uint8).reshape(k // 512, 16, n))


def unpack_fp4(words, scales):
    g, _, n = scales.shape
    words = np.ascontiguousarray(words).reshape(g, 128, n, 2)
    nib = np.empty((g, 128, n, 4), np.uint8)
    nib[..., 0::2] = words & 0xF
    nib[..., 1::2] = words >> 4
    vals = E2M1[nib] * np.repeat(np.exp2(scales.astype(np.float64) - 127.0), 8, axis=1)[..., None]
    return vals.transpose(0, 1, 3, 2).reshape(g * 512, n)


def relu(v):
    return np.maximum(v, 0.0)

def planes(y):
    n, m = y.shape
    v = y.astype(np.float32).astype(ml_dtypes.bfloat16).astype(np.float64).reshape(n // 32, 32, m)
    top = np.abs(v).max(1)
    byte = np.clip(np.where(top > 0, np.frexp(top)[1] - 1 + 127 - 7, 1), 1, 254)
    codes = (v * np.exp2(127.0 - byte)[:, None, :]).reshape(n, m).astype(np.float32).astype(ml_dtypes.float8_e4m3fn).view(np.uint8)
    words = codes.reshape(n // 512, 128, 4, m).transpose(0, 1, 3, 2)
    return np.ascontiguousarray(words), np.ascontiguousarray(byte.astype(np.uint8).reshape(n // 512, 16, m))


K, T, S, N, H = 512, 2048, 512, 512, 512
P = 2 ** 7


def setup_inputs():
    n = np.random.standard_normal
    s = mx_kscale(K)[:, None]
    u = mx_kscale(H)
    packed_xT = pack_weight(n((K, T)) * s)
    packed_w2 = pack_fp4(n((H, N)) / np.sqrt(2 * H) / u[:, None])
    packed_w3 = pack_fp4(n((H, N)) / np.sqrt(2 * H) / u[:, None])
    return {
        "x_words": packed_xT[0],
        "x_scales": packed_xT[1],
        "w1": (n((K, H)) / np.sqrt(K) / s * u).astype(np.float32),
        "k11": np.tile(np.random.uniform(0.2, 1.0, S), (P, 1)).astype(np.float32),
        "k12": np.tile(np.random.uniform(0.2, 1.0, S), (P, 1)).astype(np.float32),
        "k21": np.tile(np.random.uniform(0.2, 1.0, S), (P, 1)).astype(np.float32),
        "k22": np.tile(np.random.uniform(0.2, 1.0, S), (P, 1)).astype(np.float32),
        "w2_words": packed_w2[0],
        "w2_scales": packed_w2[1],
        "w3_words": packed_w3[0],
        "w3_scales": packed_w3[1],
        "offs": striped(np.random.permutation(T)[:S]),
        "p1": striped8(np.stack([np.random.permutation(S) for _ in range(8)])),
        "p2": striped8(np.stack([np.random.permutation(S) for _ in range(8)])),
    }


def reference(x_words, x_scales, w1, k11, k12, k21, k22, w2_words, w2_scales, w3_words, w3_scales, offs, p1, p2):
    xq = unpack_weight(x_words, x_scales)[:, unstriped(offs)]
    y = relu(mxq(f64(w1), 0, "e4m3").T @ xq)
    z = f64(k11)[:1] * (y[np.arange(H)[:, None], runs(p1, H)]) + f64(k12)[:1] * (y[np.arange(H)[:, None], runs(p2, H)])
    z2 = f64(k21)[:1] * (y[np.arange(H)[:, None], runs(p1, H)]) + f64(k22)[:1] * (y[np.arange(H)[:, None], runs(p2, H)])
    out_0 = unpack_fp4(w2_words, w2_scales).T @ mxq(z, 0, "e4m3") + unpack_fp4(w3_words, w3_scales).T @ mxq(z2, 0, "e4m3")
    return (out_0,) + planes(out_0)

@@ -1,0 +1,213 @@
+from contextlib import ExitStack
+
+import concourse.mybir as mybir
+from concourse.masks import make_identity
+
+FLOPS = 805306368
+
+F32 = mybir.dt.float32
+BF16 = mybir.dt.bfloat16
+I32 = mybir.dt.int32
+U32 = mybir.dt.uint32
+U16 = mybir.dt.uint16
+U8 = mybir.dt.uint8
+FP8X4 = mybir.dt.float8_e4m3fn_x4
+FP4X4 = mybir.dt.float4_e2m1fn_x4
+MULT = mybir.AluOpType.mult
+ADD = mybir.AluOpType.add
+COPY = mybir.ActivationFunctionType.Copy
+RELU = mybir.ActivationFunctionType.Relu
+
+P = 128
+PACK = 4
+T = 2048
+S = 512
+H = 512
+BLK = 128
+NBLK = S // BLK
+
+
+def tile_picked_kpconv2_relu_po_kernel(
+    tc, x_words, x_scales, w1, k11, k12, k21, k22, w2_words, w2_scales, w3_words, w3_scales, offs, p1, p2, out_0, out_1, out_2
+):
+    nc = tc.nc
+    with ExitStack() as ctx:
+        keep = ctx.enter_context(tc.tile_pool(name="keep", bufs=1))
+        work = ctx.enter_context(tc.tile_pool(name="work", bufs=3))
+        wide = ctx.enter_context(tc.psum_pool(name="wide", bufs=7))
+        pair = ctx.enter_context(tc.psum_pool(name="pair", bufs=1))
+
+        offs_t = keep.tile([P, S // 16], U16, name="offs_t")
+        p1_t = keep.tile([P, S // 16], U16, name="p1_t")
+        p2_t = keep.tile([P, S // 16], U16, name="p2_t")
+        xw = keep.tile([P, T], U32, name="xw", align_bytes=64)
+        xs = keep.tile([P, T], U8, name="xs", align_bytes=64)
+        w1_raw = [keep.tile([P, PACK, H // 2], F32, name="w1_raw%d" % h, align_bytes=64) for h in range(2)]
+        ww_raw = [keep.tile([P, 2 * H], U8, name="ww_raw%d" % w, align_bytes=64) for w in range(2)]
+        ws_raw = keep.tile([P, 2 * H], U8, name="ws_raw", align_bytes=64)
+        k_rows = keep.tile([P, P], F32, name="k_rows", align_bytes=64)
+        ident = keep.tile([P, P], F32, name="ident", align_bytes=64)
+
+        nc.vector.memset(xs[:].bitcast(I32), 0)
+        nc.gpsimd.memset(k_rows[:], 0.0)
+        nc.gpsimd.memset(ws_raw[:].bitcast(I32), 0)
+        make_identity(nc, ident[:])
+
+        w1_v = w1.rearrange("(p j) c -> p j c", j=PACK)
+        nc.sync.dma_start(offs_t[:], offs)
+        nc.sync.dma_start(w1_raw[0][:], w1_v[:, :, 0 : H // 2])
+        nc.sync.dma_start(w1_raw[1][:], w1_v[:, :, H // 2 : H])
+        nc.sync.dma_start(xw[:].bitcast(I32), x_words[0].rearrange("p n t -> p (n t)").bitcast(I32))
+        for q in range(4):
+            nc.scalar.dma_start(xs[32 * q : 32 * q + 4, :].bitcast(I32), x_scales[0][4 * q : 4 * q + 4, :].bitcast(I32))
+        nc.sync.dma_start(p1_t[:], p1)
+        nc.sync.dma_start(p2_t[:], p2)
+        for w, words in enumerate((w2_words, w3_words)):
+            nc.sync.dma_start(ww_raw[w][:].bitcast(I32), words[0].bitcast(I32))
+        for w, scales in enumerate((w2_scales, w3_scales)):
+            for q in range(4):
+                nc.sync.dma_start(
+                    ws_raw[32 * q : 32 * q + 4, H * w : H * (w + 1)].bitcast(I32), scales[0][4 * q : 4 * q + 4, :].bitcast(I32)
+                )
+        for i, k in enumerate((k11, k12, k21, k22)):
+            nc.sync.dma_start(k_rows[NBLK * i : NBLK * (i + 1), :], k[0:1, :].rearrange("o (b c) -> (o b) c", b=NBLK))
+
+        w1_bf = keep.tile([P, PACK * H], BF16, name="w1_bf", align_bytes=64)
+        w1_dst = w1_bf[:].rearrange("p (t m j) -> p m j t", t=PACK, j=PACK)
+        nc.scalar.copy(w1_dst[:, 0:64], w1_raw[0][:].rearrange("p j (m t) -> p m j t", t=PACK))
+        xs_g = keep.tile([P, S], U8, name="xs_g", align_bytes=64)
+        nc.vector.tensor_copy(xs_g[:], xs[:].indirect(offs_t[:]))
+        nc.vector.tensor_copy(w1_dst[:, 64:128], w1_raw[1][:].rearrange("p j (m t) -> p m j t", t=PACK))
+        w1_c = keep.tile([P, H], U32, name="w1_c", align_bytes=64)
+        w1_s = keep.tile([P, H], U8, name="w1_s", align_bytes=64)
+        nc.vector.quantize_mx(w1_c[:].bitcast(FP8X4), w1_s[:], w1_bf[:])
+        xw_g = keep.tile([P, S], U32, name="xw_g", align_bytes=64)
+        for h in range(2):
+            nc.vector.tensor_copy(xw_g[:, 256 * h : 256 * (h + 1)], xw[:].indirect(offs_t[:, 16 * h : 16 * (h + 1)]))
+
+        y = []
+        for t in range(PACK):
+            cols = slice(P * t, P * (t + 1))
+            y_ps = wide.tile([P, S], F32, name="y_ps", tag="wide")
+            y_t = keep.tile([P, S], F32, name="y%d" % t, align_bytes=64)
+            for pts in [slice(0, 256), slice(256, 512)] if t == 0 else [slice(0, 512)]:
+                nc.tensor.matmul_mx(
+                    y_ps[:, pts], w1_c[:, cols].bitcast(FP8X4), w1_s[:, cols], xw_g[:, pts].bitcast(FP8X4), xs_g[:, pts], start=True, stop=True
+                )
+                nc.scalar.activation(y_t[:, pts], y_ps[:, pts], RELU)
+            y.append(y_t)
+
+        ww = []
+        for w in range(2):
+            dealt = keep.tile([P, 2 * H], U8, name="ww%d" % w, align_bytes=64)
+            nc.vector.tensor_copy(
+                dealt[:].rearrange("p (t m e) -> p m t e", t=PACK, e=2), ww_raw[w][:].rearrange("p (m t e) -> p m t e", t=PACK, e=2)
+            )
+            ww.append(dealt)
+
+        k_ps = pair.tile([P, P], F32, name="k_ps", tag="back")
+        nc.tensor.transpose(k_ps[:], k_rows[:], ident[:])
+        k_col = keep.tile([P, 4 * NBLK], F32, name="k_col")
+        nc.scalar.copy(k_col[:], k_ps[:, 0 : 4 * NBLK])
+
+        ws = keep.tile([P, 2 * H], U8, name="ws", align_bytes=64)
+        oc = keep.tile([P, S], U32, name="oc", align_bytes=64)
+        os_ = keep.tile([P, S], U8, name="os_", align_bytes=64)
+        out0_v = out_0.rearrange("(p t) j -> p t j", t=PACK)
+        out1_v = out_1[0].rearrange("p n t -> p (n t)").bitcast(I32)
+
+        def look_up(blocks, tags):
+            width = BLK * len(blocks)
+            banks = {b: [wide.tile([P, PACK, P], F32, name="gT%d" % n, tag="wide") for n in range(2)] for b in blocks}
+            g = None
+            for t in range(PACK):
+                if tags[t] is not None:
+                    g = keep.tile([P, 2 * PACK * BLK], F32, name="g", tag=tags[t], align_bytes=64)
+                    used = 0
+                for n, lst in enumerate((p1_t, p2_t)):
+                    dst = g[:, used : used + width]
+                    used = used + width
+                    nc.vector.tensor_copy(dst, y[t][:].indirect(lst[:, BLK // 16 * blocks[0] : BLK // 16 * (blocks[-1] + 1)]))
+                    for i, b in enumerate(blocks):
+                        nc.tensor.transpose(banks[b][n][:, t, :], dst[:, BLK * i : BLK * (i + 1)], ident[:])
+            return banks
+
+        def combine(b, banks):
+            back = pair.tile([P, 2, 2, BLK], F32, name="back", tag="back")
+            both = keep.tile([P, 2 * H], F32, name="both", tag="first%d" % b, align_bytes=64)
+            for z in range(2):
+                first = both[:, H * z : H * (z + 1)]
+                c1 = NBLK * (2 * z) + b
+                c2 = NBLK * (2 * z + 1) + b
+                nc.scalar.activation(
+                    first.rearrange("j (u p e) -> j u p e", u=2, e=2),
+                    banks[0][:].rearrange("j (u e) p -> j u p e", e=2),
+                    COPY,
+                    scale=k_col[:, c1 : c1 + 1],
+                )
+                zT = work.tile([P, H], BF16, name="zT%d" % z, align_bytes=64)
+                for u in range(2):
+                    half = slice(256 * u, 256 * (u + 1))
+                    nc.vector.scalar_tensor_tensor(
+                        zT[:, half].rearrange("j (p e) -> j p e", e=2),
+                        banks[1][:, 2 * u : 2 * u + 2, :].rearrange("j e p -> j p e"),
+                        k_col[:, c2 : c2 + 1],
+                        first[:, half].rearrange("j (p e) -> j p e", e=2),
+                        MULT,
+                        ADD,
+                    )
+                    nc.tensor.transpose(back[:, z, u, :], zT[:, half].bitcast(F32), ident[:])
+            z_bf = work.tile([P, 2 * BLK * PACK], BF16, name="z_bf", align_bytes=64)
+            nc.scalar.copy(z_bf[:].bitcast(F32).rearrange("p (z j u) -> p z j u", z=2, u=2), back[:].rearrange("p z u j -> p z j u"))
+            return z_bf
+
+        def product(b, z_bf):
+            z_c = work.tile([P, 2 * BLK], U32, name="z_c", align_bytes=64)
+            z_s = work.tile([P, 2 * BLK], U8, name="z_s", align_bytes=64)
+            nc.vector.quantize_mx(z_c[:].bitcast(FP8X4), z_s[:], z_bf[:])
+            acc = wide.tile([P, PACK, BLK], F32, name="acc", tag="wide")
+            for t in range(PACK):
+                for z in range(2):
+                    nc.tensor.matmul_mx(
+                        acc[:, t, :],
+                        ww[z][:, 2 * P * t : 2 * P * (t + 1)].bitcast(FP4X4),
+                        ws[:, H * z + P * t : H * z + P * (t + 1)],
+                        z_c[:, BLK * z : BLK * (z + 1)].bitcast(FP8X4),
+                        z_s[:, BLK * z : BLK * (z + 1)],
+                        start=(z == 0),
+                        stop=(z == 1),
+                    )
+            return acc
+
+        def hand_out(b, acc):
+            cols = slice(BLK * b, BLK * (b + 1))
+            o32 = work.tile([P, PACK, BLK], F32, name="o32", align_bytes=64)
+            nc.scalar.copy(o32[:], acc[:])
+            nc.sync.dma_start(out0_v[:, :, cols], o32[:])
+            o_bf = work.tile([P, BLK * PACK], BF16, name="o_bf", align_bytes=64)
+            if b < NBLK - 1:
+                nc.scalar.copy(o_bf[:].rearrange("p (j t) -> p j t", t=PACK), acc[:].rearrange("p t j -> p j t"))
+            else:
+                nc.vector.tensor_copy(o_bf[:].rearrange("p (j t) -> p j t", t=PACK), o32[:].rearrange("p t j -> p j t"))
+            nc.vector.quantize_mx(oc[:, cols].bitcast(FP8X4), os_[:, cols], o_bf[:])
+            nc.sync.dma_start(out1_v[:, cols], oc[:, cols].bitcast(I32))
+
+        banks = look_up([0, 1], ["ga", "gb", "gc", "gd"])
+        nc.vector.tensor_copy(
+            ws[:].rearrange("p (w t m) -> p w m t", w=2, t=PACK), ws_raw[:].rearrange("p (w m t) -> p w m t", w=2, t=PACK)
+        )
+        banks.update(look_up([2], ["gc", None, None, None]))
+        z_bf = {b: combine(b, banks[b]) for b in (0, 1)}
+        acc = {0: product(0, z_bf[0])}
+        banks.update(look_up([3], ["first1", None, None, None]))
+        z_bf[2] = combine(2, banks[2])
+        acc[1] = product(1, z_bf[1])
+        hand_out(0, acc[0])
+        z_bf[3] = combine(3, banks[3])
+        acc[2] = product(2, z_bf[2])
+        hand_out(1, acc[1])
+        acc[3] = product(3, z_bf[3])
+        hand_out(2, acc[2])
+        hand_out(3, acc[3])
+        for q in range(4):
+            nc.scalar.dma_start(out_2[0][4 * q : 4 * q + 4, :].bitcast(I32), os_[32 * q : 32 * q + 4, :].bitcast(I32))

@@ -33,8 +33,7 @@ def tile_picked_kpconv2_relu_po_kernel(
     nc = tc.nc
     with ExitStack() as ctx:
         keep = ctx.enter_context(tc.tile_pool(name="keep", bufs=1))
-        work = ctx.enter_context(tc.tile_pool(name="work", bufs=3))
-        wide = ctx.enter_context(tc.psum_pool(name="wide", bufs=7))
+        work = ctx.enter_context(tc.tile_pool(name="work", bufs=6))
         pair = ctx.enter_context(tc.psum_pool(name="pair", bufs=1))
 
         offs_t = keep.tile([P, S // 16], U16, name="offs_t")
@@ -42,42 +41,39 @@ def tile_picked_kpconv2_relu_po_kernel(
         p2_t = keep.tile([P, S // 16], U16, name="p2_t")
         xw = keep.tile([P, T], U32, name="xw", align_bytes=64)
         xs = keep.tile([P, T], U8, name="xs", align_bytes=64)
-        w1_raw = [keep.tile([P, PACK, H // 2], F32, name="w1_raw%d" % h, align_bytes=64) for h in range(2)]
+        w1_raw = keep.tile([P, PACK, H], F32, name="w1_raw", align_bytes=64)
         ww_raw = [keep.tile([P, 2 * H], U8, name="ww_raw%d" % w, align_bytes=64) for w in range(2)]
         ws_raw = keep.tile([P, 2 * H], U8, name="ws_raw", align_bytes=64)
         k_rows = keep.tile([P, P], F32, name="k_rows", align_bytes=64)
         ident = keep.tile([P, P], F32, name="ident", align_bytes=64)
 
-        nc.vector.memset(xs[:].bitcast(I32), 0)
-        nc.gpsimd.memset(k_rows[:], 0.0)
-        nc.gpsimd.memset(ws_raw[:].bitcast(I32), 0)
+        nc.gpsimd.memset(xs[:].bitcast(I32), 0)
+        nc.vector.memset(ws_raw[:].bitcast(I32), 0)
+        nc.vector.memset(k_rows[:], 0.0)
         make_identity(nc, ident[:])
 
         w1_v = w1.rearrange("(p j) c -> p j c", j=PACK)
-        nc.sync.dma_start(offs_t[:], offs)
-        nc.sync.dma_start(w1_raw[0][:], w1_v[:, :, 0 : H // 2])
-        nc.sync.dma_start(w1_raw[1][:], w1_v[:, :, H // 2 : H])
-        nc.sync.dma_start(xw[:].bitcast(I32), x_words[0].rearrange("p n t -> p (n t)").bitcast(I32))
-        for q in range(4):
-            nc.scalar.dma_start(xs[32 * q : 32 * q + 4, :].bitcast(I32), x_scales[0][4 * q : 4 * q + 4, :].bitcast(I32))
-        nc.sync.dma_start(p1_t[:], p1)
-        nc.sync.dma_start(p2_t[:], p2)
         for w, words in enumerate((w2_words, w3_words)):
             nc.sync.dma_start(ww_raw[w][:].bitcast(I32), words[0].bitcast(I32))
+        nc.sync.dma_start(w1_raw[:], w1_v)
+        nc.sync.dma_start(offs_t[:], offs)
+        for q in range(4):
+            nc.sync.dma_start(xs[32 * q : 32 * q + 4, :].bitcast(I32), x_scales[0][4 * q : 4 * q + 4, :].bitcast(I32))
+        nc.sync.dma_start(xw[:].bitcast(I32), x_words[0].rearrange("p n t -> p (n t)").bitcast(I32))
         for w, scales in enumerate((w2_scales, w3_scales)):
-            for q in range(4):
-                nc.sync.dma_start(
-                    ws_raw[32 * q : 32 * q + 4, H * w : H * (w + 1)].bitcast(I32), scales[0][4 * q : 4 * q + 4, :].bitcast(I32)
-                )
+            nc.sync.dma_start(ws_raw[0:16, H * w : H * (w + 1)].bitcast(I32), scales[0].bitcast(I32))
+        nc.sync.dma_start(p1_t[:], p1)
+        nc.sync.dma_start(p2_t[:], p2)
         for i, k in enumerate((k11, k12, k21, k22)):
-            nc.sync.dma_start(k_rows[NBLK * i : NBLK * (i + 1), :], k[0:1, :].rearrange("o (b c) -> (o b) c", b=NBLK))
+            nc.gpsimd.dma_start(k_rows[NBLK * i : NBLK * (i + 1), :], k[0:1, :].rearrange("o (b c) -> (o b) c", b=NBLK))
 
         w1_bf = keep.tile([P, PACK * H], BF16, name="w1_bf", align_bytes=64)
         w1_dst = w1_bf[:].rearrange("p (t m j) -> p m j t", t=PACK, j=PACK)
-        nc.scalar.copy(w1_dst[:, 0:64], w1_raw[0][:].rearrange("p j (m t) -> p m j t", t=PACK))
+        w1_src = w1_raw[:].rearrange("p j (m t) -> p m j t", t=PACK)
+        nc.scalar.copy(w1_dst[:, 0:80], w1_src[:, 0:80])
         xs_g = keep.tile([P, S], U8, name="xs_g", align_bytes=64)
         nc.vector.tensor_copy(xs_g[:], xs[:].indirect(offs_t[:]))
-        nc.vector.tensor_copy(w1_dst[:, 64:128], w1_raw[1][:].rearrange("p j (m t) -> p m j t", t=PACK))
+        nc.vector.tensor_copy(w1_dst[:, 80:128], w1_src[:, 80:128])
         w1_c = keep.tile([P, H], U32, name="w1_c", align_bytes=64)
         w1_s = keep.tile([P, H], U8, name="w1_s", align_bytes=64)
         nc.vector.quantize_mx(w1_c[:].bitcast(FP8X4), w1_s[:], w1_bf[:])
@@ -88,7 +84,7 @@ def tile_picked_kpconv2_relu_po_kernel(
         y = []
         for t in range(PACK):
             cols = slice(P * t, P * (t + 1))
-            y_ps = wide.tile([P, S], F32, name="y_ps", tag="wide")
+            y_ps = pair.tile([P, S], F32, name="y_ps", tag="B%d" % t)
             y_t = keep.tile([P, S], F32, name="y%d" % t, align_bytes=64)
             for pts in [slice(0, 256), slice(256, 512)] if t == 0 else [slice(0, 512)]:
                 nc.tensor.matmul_mx(
@@ -97,32 +93,41 @@ def tile_picked_kpconv2_relu_po_kernel(
                 nc.scalar.activation(y_t[:, pts], y_ps[:, pts], RELU)
             y.append(y_t)
 
+        ws = keep.tile([P, 2 * H], U8, name="ws", align_bytes=64)
+        nc.vector.tensor_copy(
+            ws[:].rearrange("p (w t c m) -> p w c t m", w=2, t=PACK, m=16),
+            ws_raw[:].rearrange("p (w c m t) -> p w c t m", w=2, t=PACK, m=16),
+        )
+        for q in range(1, 4):
+            nc.sync.dma_start(ws[32 * q : 32 * q + 4, :].bitcast(I32), ws[4 * q : 4 * q + 4, :].bitcast(I32))
         ww = []
         for w in range(2):
             dealt = keep.tile([P, 2 * H], U8, name="ww%d" % w, align_bytes=64)
             nc.vector.tensor_copy(
-                dealt[:].rearrange("p (t m e) -> p m t e", t=PACK, e=2), ww_raw[w][:].rearrange("p (m t e) -> p m t e", t=PACK, e=2)
+                dealt[:].rearrange("p (t c m e) -> p c t m e", t=PACK, m=8, e=2),
+                ww_raw[w][:].rearrange("p (c m t e) -> p c t m e", t=PACK, m=8, e=2),
             )
             ww.append(dealt)
 
-        k_ps = pair.tile([P, P], F32, name="k_ps", tag="back")
+        k_ps = pair.tile([P, P], F32, name="k_ps", tag="B7")
         nc.tensor.transpose(k_ps[:], k_rows[:], ident[:])
         k_col = keep.tile([P, 4 * NBLK], F32, name="k_col")
         nc.scalar.copy(k_col[:], k_ps[:, 0 : 4 * NBLK])
 
-        ws = keep.tile([P, 2 * H], U8, name="ws", align_bytes=64)
         oc = keep.tile([P, S], U32, name="oc", align_bytes=64)
         os_ = keep.tile([P, S], U8, name="os_", align_bytes=64)
         out0_v = out_0.rearrange("(p t) j -> p t j", t=PACK)
         out1_v = out_1[0].rearrange("p n t -> p (n t)").bitcast(I32)
 
-        def look_up(blocks, tags):
+        def look_up(blocks, tags, bank_tags):
             width = BLK * len(blocks)
-            banks = {b: [wide.tile([P, PACK, P], F32, name="gT%d" % n, tag="wide") for n in range(2)] for b in blocks}
+            banks = {
+                b: [pair.tile([P, PACK, P], F32, name="gT%d" % n, tag=bank_tags[2 * i + n]) for n in range(2)] for i, b in enumerate(blocks)
+            }
             g = None
             for t in range(PACK):
                 if tags[t] is not None:
-                    g = keep.tile([P, 2 * PACK * BLK], F32, name="g", tag=tags[t], align_bytes=64)
+                    g = keep.tile([P, 2 * PACK * width], F32, name="g", tag=tags[t], align_bytes=64)
                     used = 0
                 for n, lst in enumerate((p1_t, p2_t)):
                     dst = g[:, used : used + width]
@@ -132,82 +137,128 @@ def tile_picked_kpconv2_relu_po_kernel(
                         nc.tensor.transpose(banks[b][n][:, t, :], dst[:, BLK * i : BLK * (i + 1)], ident[:])
             return banks
 
-        def combine(b, banks):
-            back = pair.tile([P, 2, 2, BLK], F32, name="back", tag="back")
-            both = keep.tile([P, 2 * H], F32, name="both", tag="first%d" % b, align_bytes=64)
-            for z in range(2):
-                first = both[:, H * z : H * (z + 1)]
-                c1 = NBLK * (2 * z) + b
-                c2 = NBLK * (2 * z + 1) + b
-                nc.scalar.activation(
-                    first.rearrange("j (u p e) -> j u p e", u=2, e=2),
-                    banks[0][:].rearrange("j (u e) p -> j u p e", e=2),
-                    COPY,
-                    scale=k_col[:, c1 : c1 + 1],
+        def weigh(dst, bank, col):
+            nc.scalar.activation(
+                dst.rearrange("j (u p e) -> j u p e", u=2, e=2),
+                bank[:].rearrange("j (u e) p -> j u p e", e=2),
+                COPY,
+                scale=k_col[:, col : col + 1],
+            )
+
+        def mix(b, z, banks):
+            c1 = NBLK * (2 * z) + b
+            c2 = NBLK * (2 * z + 1) + b
+            first = work.tile([P, H], F32, name="first", align_bytes=64)
+            weigh(first[:], banks[0], c1)
+            zT = work.tile([P, H], BF16, name="zT", align_bytes=64)
+            for u in range(2):
+                half = slice(256 * u, 256 * (u + 1))
+                nc.vector.scalar_tensor_tensor(
+                    zT[:, half].rearrange("j (p e) -> j p e", e=2),
+                    banks[1][:, 2 * u : 2 * u + 2, :].rearrange("j e p -> j p e"),
+                    k_col[:, c2 : c2 + 1],
+                    first[:, half].rearrange("j (p e) -> j p e", e=2),
+                    MULT,
+                    ADD,
                 )
-                zT = work.tile([P, H], BF16, name="zT%d" % z, align_bytes=64)
+            return zT
+
+        def turn_back(zTs, bank_tag):
+            n = len(zTs)
+            back = pair.tile([P, n, 2, BLK], F32, name="back", tag=bank_tag)
+            for z, zT in enumerate(zTs):
                 for u in range(2):
-                    half = slice(256 * u, 256 * (u + 1))
-                    nc.vector.scalar_tensor_tensor(
-                        zT[:, half].rearrange("j (p e) -> j p e", e=2),
-                        banks[1][:, 2 * u : 2 * u + 2, :].rearrange("j e p -> j p e"),
-                        k_col[:, c2 : c2 + 1],
-                        first[:, half].rearrange("j (p e) -> j p e", e=2),
-                        MULT,
-                        ADD,
-                    )
-                    nc.tensor.transpose(back[:, z, u, :], zT[:, half].bitcast(F32), ident[:])
-            z_bf = work.tile([P, 2 * BLK * PACK], BF16, name="z_bf", align_bytes=64)
-            nc.scalar.copy(z_bf[:].bitcast(F32).rearrange("p (z j u) -> p z j u", z=2, u=2), back[:].rearrange("p z u j -> p z j u"))
+                    nc.tensor.transpose(back[:, z, u, :], zT[:, 256 * u : 256 * (u + 1)].bitcast(F32), ident[:])
+            z_bf = work.tile([P, n * BLK * PACK], BF16, name="z_bf", align_bytes=64)
+            nc.scalar.copy(z_bf[:].bitcast(F32).rearrange("p (z j u) -> p z j u", z=n, u=2), back[:].rearrange("p z u j -> p z j u"))
             return z_bf
 
-        def product(b, z_bf):
-            z_c = work.tile([P, 2 * BLK], U32, name="z_c", align_bytes=64)
-            z_s = work.tile([P, 2 * BLK], U8, name="z_s", align_bytes=64)
+        def mix_in_psum(b, banks, bank_tags):
+            z_bf = work.tile([P, 2 * BLK * PACK], BF16, name="z_bf", align_bytes=64)
+            for z in range(2):
+                total = pair.tile([P, PACK, BLK], F32, name="total", tag=bank_tags[z])
+                terms = []
+                for n in range(2):
+                    term = work.tile([P, PACK, P], F32, name="first", align_bytes=64)
+                    col = NBLK * (2 * z + n) + b
+                    nc.scalar.activation(term[:], banks[n][:], COPY, scale=k_col[:, col : col + 1])
+                    terms.append(term)
+                for t in range(PACK):
+                    for n in range(2):
+                        nc.tensor.matmul(total[:, t, :], terms[n][:, t, :], ident[:], start=(n == 0), stop=(n == 1), is_transpose=True)
+                nc.scalar.copy(
+                    z_bf[:, BLK * PACK * z : BLK * PACK * (z + 1)].rearrange("p (j t) -> p j t", t=PACK), total[:].rearrange("p t j -> p j t")
+                )
+            return z_bf
+
+        def quantise(z_bf, n):
+            z_c = work.tile([P, n * BLK], U32, name="z_c", align_bytes=64)
+            z_s = work.tile([P, n * BLK], U8, name="z_s", align_bytes=64)
             nc.vector.quantize_mx(z_c[:].bitcast(FP8X4), z_s[:], z_bf[:])
-            acc = wide.tile([P, PACK, BLK], F32, name="acc", tag="wide")
+            return [(z_c[:, BLK * z : BLK * (z + 1)], z_s[:, BLK * z : BLK * (z + 1)]) for z in range(n)]
+
+        def one_pass(dst, t, z, operand):
+            nc.tensor.matmul_mx(
+                dst,
+                ww[z][:, 2 * P * t : 2 * P * (t + 1)].bitcast(FP4X4),
+                ws[:, H * z + P * t : H * z + P * (t + 1)],
+                operand[0].bitcast(FP8X4),
+                operand[1],
+                start=(z == 0),
+                stop=(z == 1),
+            )
+
+        def product(z_bf, bank_tag):
+            operands = quantise(z_bf, 2)
+            acc = pair.tile([P, PACK, BLK], F32, name="acc", tag=bank_tag)
             for t in range(PACK):
                 for z in range(2):
-                    nc.tensor.matmul_mx(
-                        acc[:, t, :],
-                        ww[z][:, 2 * P * t : 2 * P * (t + 1)].bitcast(FP4X4),
-                        ws[:, H * z + P * t : H * z + P * (t + 1)],
-                        z_c[:, BLK * z : BLK * (z + 1)].bitcast(FP8X4),
-                        z_s[:, BLK * z : BLK * (z + 1)],
-                        start=(z == 0),
-                        stop=(z == 1),
-                    )
+                    one_pass(acc[:, t, :], t, z, operands[z])
             return acc
 
-        def hand_out(b, acc):
+        def planes(b, o32):
             cols = slice(BLK * b, BLK * (b + 1))
-            o32 = work.tile([P, PACK, BLK], F32, name="o32", align_bytes=64)
-            nc.scalar.copy(o32[:], acc[:])
-            nc.sync.dma_start(out0_v[:, :, cols], o32[:])
             o_bf = work.tile([P, BLK * PACK], BF16, name="o_bf", align_bytes=64)
-            if b < NBLK - 1:
-                nc.scalar.copy(o_bf[:].rearrange("p (j t) -> p j t", t=PACK), acc[:].rearrange("p t j -> p j t"))
-            else:
-                nc.vector.tensor_copy(o_bf[:].rearrange("p (j t) -> p j t", t=PACK), o32[:].rearrange("p t j -> p j t"))
+            nc.vector.tensor_copy(o_bf[:].rearrange("p (j t) -> p j t", t=PACK), o32[:].rearrange("p t j -> p j t"))
             nc.vector.quantize_mx(oc[:, cols].bitcast(FP8X4), os_[:, cols], o_bf[:])
             nc.sync.dma_start(out1_v[:, cols], oc[:, cols].bitcast(I32))
 
-        banks = look_up([0, 1], ["ga", "gb", "gc", "gd"])
-        nc.vector.tensor_copy(
-            ws[:].rearrange("p (w t m) -> p w m t", w=2, t=PACK), ws_raw[:].rearrange("p (w m t) -> p w m t", w=2, t=PACK)
-        )
-        banks.update(look_up([2], ["gc", None, None, None]))
-        z_bf = {b: combine(b, banks[b]) for b in (0, 1)}
-        acc = {0: product(0, z_bf[0])}
-        banks.update(look_up([3], ["first1", None, None, None]))
-        z_bf[2] = combine(2, banks[2])
-        acc[1] = product(1, z_bf[1])
-        hand_out(0, acc[0])
-        z_bf[3] = combine(3, banks[3])
-        acc[2] = product(2, z_bf[2])
-        hand_out(1, acc[1])
-        acc[3] = product(3, z_bf[3])
-        hand_out(2, acc[2])
-        hand_out(3, acc[3])
+        def hand_out(b, acc):
+            o32 = work.tile([P, PACK, BLK], F32, name="o32", align_bytes=64)
+            nc.scalar.copy(o32[:], acc[:])
+            nc.sync.dma_start(out0_v[:, :, BLK * b : BLK * (b + 1)], o32[:])
+            return o32
+
+        banks = look_up([0, 1], ["ga", "gb", "gc", "gd"], ("B4", "B5", "B6", "B0"))
+        z_bf = {0: mix_in_psum(0, banks[0], ("B7", "B1"))}
+        banks.update(look_up([2, 3], ["gc", None, None, None], ("B4", "B5", "B7", "B1")))
+        acc = {0: product(z_bf[0], "B2")}
+        z_bf[1] = turn_back([mix(1, z, banks[1]) for z in range(2)], "B3")
+        z_bf[2] = turn_back([mix(2, z, banks[2]) for z in range(2)], "B0")
+        acc[1] = product(z_bf[1], "B6")
+        zT3 = [mix(3, z, banks[3]) for z in range(2)]
+        result = {0: hand_out(0, acc[0])}
+        acc[2] = product(z_bf[2], "B4")
+        last = [pair.tile([P, BLK], F32, name="last", tag=tag) for tag in ("B2", "B5", "B7", "B1")]
+        operands = []
+        for z in range(2):
+            operands.append(quantise(turn_back([zT3[z]], ("B3", "B0")[z]), 1)[0])
+            for t in range(PACK - 1):
+                one_pass(last[t][:], t, z, operands[z])
+            if z == 0:
+                result[1] = hand_out(1, acc[1])
+        for z in range(2):
+            one_pass(last[3][:], 3, z, operands[z])
+        result[2] = hand_out(2, acc[2])
+        for b in range(3):
+            planes(b, result[b])
+        o32 = work.tile([P, PACK, BLK], F32, name="o32", align_bytes=64)
+        for t in range(PACK):
+            if t % 2 == 0:
+                nc.scalar.copy(o32[:, t, :], last[t][:])
+            else:
+                nc.vector.tensor_copy(o32[:, t, :], last[t][:])
+        nc.sync.dma_start(out0_v[:, :, BLK * 3 : BLK * 4], o32[:])
+        planes(3, o32)
         for q in range(4):
             nc.scalar.dma_start(out_2[0][4 * q : 4 * q + 4, :].bitcast(I32), os_[32 * q : 32 * q + 4, :].bitcast(I32))

@@ -33,13 +33,13 @@ def tile_picked_kpconv2_relu_po_kernel(
     nc = tc.nc
     with ExitStack() as ctx:
         keep = ctx.enter_context(tc.tile_pool(name="keep", bufs=1))
-        work = ctx.enter_context(tc.tile_pool(name="work", bufs=6))
+        work = ctx.enter_context(tc.tile_pool(name="work", bufs=12))
         pair = ctx.enter_context(tc.psum_pool(name="pair", bufs=1))
 
         offs_t = keep.tile([P, S // 16], U16, name="offs_t")
         p1_t = keep.tile([P, S // 16], U16, name="p1_t")
         p2_t = keep.tile([P, S // 16], U16, name="p2_t")
-        xw = keep.tile([P, T], U32, name="xw", align_bytes=64)
+        xw = keep.tile([P, T], U32, name="xw", tag="xw", align_bytes=64)
         xs = keep.tile([P, T], U8, name="xs", align_bytes=64)
         w1_raw = keep.tile([P, PACK, H], F32, name="w1_raw", align_bytes=64)
         ww_raw = [keep.tile([P, 2 * H], U8, name="ww_raw%d" % w, align_bytes=64) for w in range(2)]
@@ -50,7 +50,6 @@ def tile_picked_kpconv2_relu_po_kernel(
         nc.gpsimd.memset(xs[:].bitcast(I32), 0)
         nc.vector.memset(ws_raw[:].bitcast(I32), 0)
         nc.vector.memset(k_rows[:], 0.0)
-        make_identity(nc, ident[:])
 
         w1_v = w1.rearrange("(p j) c -> p j c", j=PACK)
         for w, words in enumerate((w2_words, w3_words)):
@@ -61,11 +60,13 @@ def tile_picked_kpconv2_relu_po_kernel(
             nc.sync.dma_start(xs[32 * q : 32 * q + 4, :].bitcast(I32), x_scales[0][4 * q : 4 * q + 4, :].bitcast(I32))
         nc.sync.dma_start(xw[:].bitcast(I32), x_words[0].rearrange("p n t -> p (n t)").bitcast(I32))
         for w, scales in enumerate((w2_scales, w3_scales)):
-            nc.sync.dma_start(ws_raw[0:16, H * w : H * (w + 1)].bitcast(I32), scales[0].bitcast(I32))
+            nc.gpsimd.dma_start(ws_raw[0:16, H * w : H * (w + 1)].bitcast(I32), scales[0].bitcast(I32))
         nc.sync.dma_start(p1_t[:], p1)
         nc.sync.dma_start(p2_t[:], p2)
         for i, k in enumerate((k11, k12, k21, k22)):
-            nc.gpsimd.dma_start(k_rows[NBLK * i : NBLK * (i + 1), :], k[0:1, :].rearrange("o (b c) -> (o b) c", b=NBLK))
+            nc.sync.dma_start(k_rows[NBLK * i : NBLK * (i + 1), :], k[0:1, :].rearrange("o (b c) -> (o b) c", b=NBLK))
+
+        make_identity(nc, ident[:])
 
         w1_bf = keep.tile([P, PACK * H], BF16, name="w1_bf", align_bytes=64)
         w1_dst = w1_bf[:].rearrange("p (t m j) -> p m j t", t=PACK, j=PACK)
@@ -84,16 +85,16 @@ def tile_picked_kpconv2_relu_po_kernel(
         y = []
         for t in range(PACK):
             cols = slice(P * t, P * (t + 1))
-            y_ps = pair.tile([P, S], F32, name="y_ps", tag="B%d" % t)
             y_t = keep.tile([P, S], F32, name="y%d" % t, align_bytes=64)
-            for pts in [slice(0, 256), slice(256, 512)] if t == 0 else [slice(0, 512)]:
+            for pts, tag in [(slice(0, 256), "B6"), (slice(256, 512), "B0")] if t == 0 else [(slice(0, 512), "B%d" % t)]:
+                y_ps = pair.tile([P, pts.stop - pts.start], F32, name="y_ps", tag=tag)
                 nc.tensor.matmul_mx(
-                    y_ps[:, pts], w1_c[:, cols].bitcast(FP8X4), w1_s[:, cols], xw_g[:, pts].bitcast(FP8X4), xs_g[:, pts], start=True, stop=True
+                    y_ps[:], w1_c[:, cols].bitcast(FP8X4), w1_s[:, cols], xw_g[:, pts].bitcast(FP8X4), xs_g[:, pts], start=True, stop=True
                 )
-                nc.scalar.activation(y_t[:, pts], y_ps[:, pts], RELU)
+                nc.scalar.activation(y_t[:, pts], y_ps[:], RELU)
             y.append(y_t)
 
-        ws = keep.tile([P, 2 * H], U8, name="ws", align_bytes=64)
+        ws = keep.tile([P, 2 * H], U8, name="ws", tag="xw", align_bytes=64)
         nc.vector.tensor_copy(
             ws[:].rearrange("p (w t c m) -> p w c t m", w=2, t=PACK, m=16),
             ws_raw[:].rearrange("p (w c m t) -> p w c t m", w=2, t=PACK, m=16),
@@ -216,12 +217,17 @@ def tile_picked_kpconv2_relu_po_kernel(
                     one_pass(acc[:, t, :], t, z, operands[z])
             return acc
 
-        def planes(b, o32):
+        def planes(b, o32, acc=None):
             cols = slice(BLK * b, BLK * (b + 1))
             o_bf = work.tile([P, BLK * PACK], BF16, name="o_bf", align_bytes=64)
-            nc.vector.tensor_copy(o_bf[:].rearrange("p (j t) -> p j t", t=PACK), o32[:].rearrange("p t j -> p j t"))
+            if acc is None:
+                nc.vector.tensor_copy(o_bf[:].rearrange("p (j t) -> p j t", t=PACK), o32[:].rearrange("p t j -> p j t"))
+            else:
+                nc.scalar.copy(o_bf[:].rearrange("p (j t) -> p j t", t=PACK), acc[:].rearrange("p t j -> p j t"))
             nc.vector.quantize_mx(oc[:, cols].bitcast(FP8X4), os_[:, cols], o_bf[:])
-            nc.sync.dma_start(out1_v[:, cols], oc[:, cols].bitcast(I32))
+            if b % 2 == 1:
+                both = slice(BLK * (b - 1), BLK * (b + 1))
+                nc.sync.dma_start(out1_v[:, both], oc[:, both].bitcast(I32))
 
         def hand_out(b, acc):
             o32 = work.tile([P, PACK, BLK], F32, name="o32", align_bytes=64)
@@ -232,26 +238,26 @@ def tile_picked_kpconv2_relu_po_kernel(
         banks = look_up([0, 1], ["ga", "gb", "gc", "gd"], ("B4", "B5", "B6", "B0"))
         z_bf = {0: mix_in_psum(0, banks[0], ("B7", "B1"))}
         banks.update(look_up([2, 3], ["gc", None, None, None], ("B4", "B5", "B7", "B1")))
+        zT1 = [mix(1, z, banks[1]) for z in range(2)]
+        zT2 = [mix(2, z, banks[2]) for z in range(2)]
+        z_bf[1] = turn_back(zT1, "B3")
         acc = {0: product(z_bf[0], "B2")}
-        z_bf[1] = turn_back([mix(1, z, banks[1]) for z in range(2)], "B3")
-        z_bf[2] = turn_back([mix(2, z, banks[2]) for z in range(2)], "B0")
-        acc[1] = product(z_bf[1], "B6")
         zT3 = [mix(3, z, banks[3]) for z in range(2)]
-        result = {0: hand_out(0, acc[0])}
+        acc[1] = product(z_bf[1], "B6")
+        z_bf[2] = turn_back(zT2, "B0")
         acc[2] = product(z_bf[2], "B4")
-        last = [pair.tile([P, BLK], F32, name="last", tag=tag) for tag in ("B2", "B5", "B7", "B1")]
-        operands = []
+        last = [pair.tile([P, BLK], F32, name="last", tag=tag) for tag in ("B5", "B7", "B1", "B2")]
+        operands, result = [], {}
         for z in range(2):
             operands.append(quantise(turn_back([zT3[z]], ("B3", "B0")[z]), 1)[0])
-            for t in range(PACK - 1):
-                one_pass(last[t][:], t, z, operands[z])
             if z == 0:
-                result[1] = hand_out(1, acc[1])
-        for z in range(2):
-            one_pass(last[3][:], 3, z, operands[z])
-        result[2] = hand_out(2, acc[2])
-        for b in range(3):
-            planes(b, result[b])
+                result[0] = hand_out(0, acc[0])
+            for t in range(PACK):
+                one_pass(last[t][:], t, z, operands[z])
+        for b in (1, 2):
+            result[b] = hand_out(b, acc[b])
+        planes(0, result[0])
+        planes(1, result[1])
         o32 = work.tile([P, PACK, BLK], F32, name="o32", align_bytes=64)
         for t in range(PACK):
             if t % 2 == 0:
@@ -259,6 +265,7 @@ def tile_picked_kpconv2_relu_po_kernel(
             else:
                 nc.vector.tensor_copy(o32[:, t, :], last[t][:])
         nc.sync.dma_start(out0_v[:, :, BLK * 3 : BLK * 4], o32[:])
+        planes(2, result[2])
         planes(3, o32)
         for q in range(4):
             nc.scalar.dma_start(out_2[0][4 * q : 4 * q + 4, :].bitcast(I32), os_[32 * q : 32 * q + 4, :].bitcast(I32))

@@ -57,7 +57,7 @@ def tile_picked_kpconv2_relu_po_kernel(
         nc.sync.dma_start(w1_raw[:], w1_v)
         nc.sync.dma_start(offs_t[:], offs)
         for q in range(4):
-            nc.sync.dma_start(xs[32 * q : 32 * q + 4, :].bitcast(I32), x_scales[0][4 * q : 4 * q + 4, :].bitcast(I32))
+            nc.scalar.dma_start(xs[32 * q : 32 * q + 4, :].bitcast(I32), x_scales[0][4 * q : 4 * q + 4, :].bitcast(I32))
         nc.sync.dma_start(xw[:].bitcast(I32), x_words[0].rearrange("p n t -> p (n t)").bitcast(I32))
         for w, scales in enumerate((w2_scales, w3_scales)):
             nc.gpsimd.dma_start(ws_raw[0:16, H * w : H * (w + 1)].bitcast(I32), scales[0].bitcast(I32))
@@ -71,10 +71,10 @@ def tile_picked_kpconv2_relu_po_kernel(
         w1_bf = keep.tile([P, PACK * H], BF16, name="w1_bf", align_bytes=64)
         w1_dst = w1_bf[:].rearrange("p (t m j) -> p m j t", t=PACK, j=PACK)
         w1_src = w1_raw[:].rearrange("p j (m t) -> p m j t", t=PACK)
-        nc.scalar.copy(w1_dst[:, 0:80], w1_src[:, 0:80])
+        nc.scalar.copy(w1_dst[:, 0:64], w1_src[:, 0:64])
         xs_g = keep.tile([P, S], U8, name="xs_g", align_bytes=64)
         nc.vector.tensor_copy(xs_g[:], xs[:].indirect(offs_t[:]))
-        nc.vector.tensor_copy(w1_dst[:, 80:128], w1_src[:, 80:128])
+        nc.vector.tensor_copy(w1_dst[:, 64:128], w1_src[:, 64:128])
         w1_c = keep.tile([P, H], U32, name="w1_c", align_bytes=64)
         w1_s = keep.tile([P, H], U8, name="w1_s", align_bytes=64)
         nc.vector.quantize_mx(w1_c[:].bitcast(FP8X4), w1_s[:], w1_bf[:])
@@ -268,4 +268,4 @@ def tile_picked_kpconv2_relu_po_kernel(
         planes(2, result[2])
         planes(3, o32)
         for q in range(4):
-            nc.scalar.dma_start(out_2[0][4 * q : 4 * q + 4, :].bitcast(I32), os_[32 * q : 32 * q + 4, :].bitcast(I32))
+            (nc.scalar, nc.sync)[q % 2].dma_start(out_2[0][4 * q : 4 * q + 4, :].bitcast(I32), os_[32 * q : 32 * q + 4, :].bitcast(I32))

from contextlib import ExitStack

import concourse.mybir as mybir
from concourse.masks import make_identity

FLOPS = 805306368

F32 = mybir.dt.float32
BF16 = mybir.dt.bfloat16
I32 = mybir.dt.int32
U32 = mybir.dt.uint32
U16 = mybir.dt.uint16
U8 = mybir.dt.uint8
FP8X4 = mybir.dt.float8_e4m3fn_x4
FP4X4 = mybir.dt.float4_e2m1fn_x4
MULT = mybir.AluOpType.mult
ADD = mybir.AluOpType.add
COPY = mybir.ActivationFunctionType.Copy
RELU = mybir.ActivationFunctionType.Relu

P = 128
PACK = 4
T = 2048
S = 512
H = 512
BLK = 128
NBLK = S // BLK


def tile_picked_kpconv2_relu_po_kernel(
    tc, x_words, x_scales, w1, k11, k12, k21, k22, w2_words, w2_scales, w3_words, w3_scales, offs, p1, p2, out_0, out_1, out_2
):
    nc = tc.nc
    with ExitStack() as ctx:
        keep = ctx.enter_context(tc.tile_pool(name="keep", bufs=1))
        work = ctx.enter_context(tc.tile_pool(name="work", bufs=12))
        pair = ctx.enter_context(tc.psum_pool(name="pair", bufs=1))

        offs_t = keep.tile([P, S // 16], U16, name="offs_t")
        p1_t = keep.tile([P, S // 16], U16, name="p1_t")
        p2_t = keep.tile([P, S // 16], U16, name="p2_t")
        xw = keep.tile([P, T], U32, name="xw", tag="xw", align_bytes=64)
        xs = keep.tile([P, T], U8, name="xs", align_bytes=64)
        w1_raw = keep.tile([P, PACK, H], F32, name="w1_raw", align_bytes=64)
        ww_raw = [keep.tile([P, 2 * H], U8, name="ww_raw%d" % w, align_bytes=64) for w in range(2)]
        ws_raw = keep.tile([P, 2 * H], U8, name="ws_raw", align_bytes=64)
        k_rows = keep.tile([P, P], F32, name="k_rows", align_bytes=64)
        ident = keep.tile([P, P], F32, name="ident", align_bytes=64)

        nc.gpsimd.memset(xs[:].bitcast(I32), 0)
        nc.vector.memset(ws_raw[:].bitcast(I32), 0)
        nc.vector.memset(k_rows[:], 0.0)

        w1_v = w1.rearrange("(p j) c -> p j c", j=PACK)
        for w, words in enumerate((w2_words, w3_words)):
            nc.sync.dma_start(ww_raw[w][:].bitcast(I32), words[0].bitcast(I32))
        nc.sync.dma_start(w1_raw[:], w1_v)
        nc.sync.dma_start(offs_t[:], offs)
        for q in range(4):
            nc.scalar.dma_start(xs[32 * q : 32 * q + 4, :].bitcast(I32), x_scales[0][4 * q : 4 * q + 4, :].bitcast(I32))
        nc.sync.dma_start(xw[:].bitcast(I32), x_words[0].rearrange("p n t -> p (n t)").bitcast(I32))
        for w, scales in enumerate((w2_scales, w3_scales)):
            nc.gpsimd.dma_start(ws_raw[0:16, H * w : H * (w + 1)].bitcast(I32), scales[0].bitcast(I32))
        nc.sync.dma_start(p1_t[:], p1)
        nc.sync.dma_start(p2_t[:], p2)
        for i, k in enumerate((k11, k12, k21, k22)):
            nc.sync.dma_start(k_rows[NBLK * i : NBLK * (i + 1), :], k[0:1, :].rearrange("o (b c) -> (o b) c", b=NBLK))

        make_identity(nc, ident[:])

        w1_bf = keep.tile([P, PACK * H], BF16, name="w1_bf", align_bytes=64)
        w1_dst = w1_bf[:].rearrange("p (t m j) -> p m j t", t=PACK, j=PACK)
        w1_src = w1_raw[:].rearrange("p j (m t) -> p m j t", t=PACK)
        nc.scalar.copy(w1_dst[:, 0:64], w1_src[:, 0:64])
        xs_g = keep.tile([P, S], U8, name="xs_g", align_bytes=64)
        nc.vector.tensor_copy(xs_g[:], xs[:].indirect(offs_t[:]))
        nc.vector.tensor_copy(w1_dst[:, 64:128], w1_src[:, 64:128])
        w1_c = keep.tile([P, H], U32, name="w1_c", align_bytes=64)
        w1_s = keep.tile([P, H], U8, name="w1_s", align_bytes=64)
        nc.vector.quantize_mx(w1_c[:].bitcast(FP8X4), w1_s[:], w1_bf[:])
        xw_g = keep.tile([P, S], U32, name="xw_g", align_bytes=64)
        for h in range(2):
            nc.vector.tensor_copy(xw_g[:, 256 * h : 256 * (h + 1)], xw[:].indirect(offs_t[:, 16 * h : 16 * (h + 1)]))

        y = []
        for t in range(PACK):
            cols = slice(P * t, P * (t + 1))
            y_t = keep.tile([P, S], F32, name="y%d" % t, align_bytes=64)
            for pts, tag in [(slice(0, 256), "B6"), (slice(256, 512), "B0")] if t == 0 else [(slice(0, 512), "B%d" % t)]:
                y_ps = pair.tile([P, pts.stop - pts.start], F32, name="y_ps", tag=tag)
                nc.tensor.matmul_mx(
                    y_ps[:], w1_c[:, cols].bitcast(FP8X4), w1_s[:, cols], xw_g[:, pts].bitcast(FP8X4), xs_g[:, pts], start=True, stop=True
                )
                nc.scalar.activation(y_t[:, pts], y_ps[:], RELU)
            y.append(y_t)

        ws = keep.tile([P, 2 * H], U8, name="ws", tag="xw", align_bytes=64)
        nc.vector.tensor_copy(
            ws[:].rearrange("p (w t c m) -> p w c t m", w=2, t=PACK, m=16),
            ws_raw[:].rearrange("p (w c m t) -> p w c t m", w=2, t=PACK, m=16),
        )
        for q in range(1, 4):
            nc.sync.dma_start(ws[32 * q : 32 * q + 4, :].bitcast(I32), ws[4 * q : 4 * q + 4, :].bitcast(I32))
        ww = []
        for w in range(2):
            dealt = keep.tile([P, 2 * H], U8, name="ww%d" % w, align_bytes=64)
            nc.vector.tensor_copy(
                dealt[:].rearrange("p (t c m e) -> p c t m e", t=PACK, m=8, e=2),
                ww_raw[w][:].rearrange("p (c m t e) -> p c t m e", t=PACK, m=8, e=2),
            )
            ww.append(dealt)

        k_ps = pair.tile([P, P], F32, name="k_ps", tag="B7")
        nc.tensor.transpose(k_ps[:], k_rows[:], ident[:])
        k_col = keep.tile([P, 4 * NBLK], F32, name="k_col")
        nc.scalar.copy(k_col[:], k_ps[:, 0 : 4 * NBLK])

        oc = keep.tile([P, S], U32, name="oc", align_bytes=64)
        os_ = keep.tile([P, S], U8, name="os_", align_bytes=64)
        out0_v = out_0.rearrange("(p t) j -> p t j", t=PACK)
        out1_v = out_1[0].rearrange("p n t -> p (n t)").bitcast(I32)

        def look_up(blocks, tags, bank_tags):
            width = BLK * len(blocks)
            banks = {
                b: [pair.tile([P, PACK, P], F32, name="gT%d" % n, tag=bank_tags[2 * i + n]) for n in range(2)] for i, b in enumerate(blocks)
            }
            g = None
            for t in range(PACK):
                if tags[t] is not None:
                    g = keep.tile([P, 2 * PACK * width], F32, name="g", tag=tags[t], align_bytes=64)
                    used = 0
                for n, lst in enumerate((p1_t, p2_t)):
                    dst = g[:, used : used + width]
                    used = used + width
                    nc.vector.tensor_copy(dst, y[t][:].indirect(lst[:, BLK // 16 * blocks[0] : BLK // 16 * (blocks[-1] + 1)]))
                    for i, b in enumerate(blocks):
                        nc.tensor.transpose(banks[b][n][:, t, :], dst[:, BLK * i : BLK * (i + 1)], ident[:])
            return banks

        def weigh(dst, bank, col):
            nc.scalar.activation(
                dst.rearrange("j (u p e) -> j u p e", u=2, e=2),
                bank[:].rearrange("j (u e) p -> j u p e", e=2),
                COPY,
                scale=k_col[:, col : col + 1],
            )

        def mix(b, z, banks):
            c1 = NBLK * (2 * z) + b
            c2 = NBLK * (2 * z + 1) + b
            first = work.tile([P, H], F32, name="first", align_bytes=64)
            weigh(first[:], banks[0], c1)
            zT = work.tile([P, H], BF16, name="zT", align_bytes=64)
            for u in range(2):
                half = slice(256 * u, 256 * (u + 1))
                nc.vector.scalar_tensor_tensor(
                    zT[:, half].rearrange("j (p e) -> j p e", e=2),
                    banks[1][:, 2 * u : 2 * u + 2, :].rearrange("j e p -> j p e"),
                    k_col[:, c2 : c2 + 1],
                    first[:, half].rearrange("j (p e) -> j p e", e=2),
                    MULT,
                    ADD,
                )
            return zT

        def turn_back(zTs, bank_tag):
            n = len(zTs)
            back = pair.tile([P, n, 2, BLK], F32, name="back", tag=bank_tag)
            for z, zT in enumerate(zTs):
                for u in range(2):
                    nc.tensor.transpose(back[:, z, u, :], zT[:, 256 * u : 256 * (u + 1)].bitcast(F32), ident[:])
            z_bf = work.tile([P, n * BLK * PACK], BF16, name="z_bf", align_bytes=64)
            nc.scalar.copy(z_bf[:].bitcast(F32).rearrange("p (z j u) -> p z j u", z=n, u=2), back[:].rearrange("p z u j -> p z j u"))
            return z_bf

        def mix_in_psum(b, banks, bank_tags):
            z_bf = work.tile([P, 2 * BLK * PACK], BF16, name="z_bf", align_bytes=64)
            for z in range(2):
                total = pair.tile([P, PACK, BLK], F32, name="total", tag=bank_tags[z])
                terms = []
                for n in range(2):
                    term = work.tile([P, PACK, P], F32, name="first", align_bytes=64)
                    col = NBLK * (2 * z + n) + b
                    nc.scalar.activation(term[:], banks[n][:], COPY, scale=k_col[:, col : col + 1])
                    terms.append(term)
                for t in range(PACK):
                    for n in range(2):
                        nc.tensor.matmul(total[:, t, :], terms[n][:, t, :], ident[:], start=(n == 0), stop=(n == 1), is_transpose=True)
                nc.scalar.copy(
                    z_bf[:, BLK * PACK * z : BLK * PACK * (z + 1)].rearrange("p (j t) -> p j t", t=PACK), total[:].rearrange("p t j -> p j t")
                )
            return z_bf

        def quantise(z_bf, n):
            z_c = work.tile([P, n * BLK], U32, name="z_c", align_bytes=64)
            z_s = work.tile([P, n * BLK], U8, name="z_s", align_bytes=64)
            nc.vector.quantize_mx(z_c[:].bitcast(FP8X4), z_s[:], z_bf[:])
            return [(z_c[:, BLK * z : BLK * (z + 1)], z_s[:, BLK * z : BLK * (z + 1)]) for z in range(n)]

        def one_pass(dst, t, z, operand):
            nc.tensor.matmul_mx(
                dst,
                ww[z][:, 2 * P * t : 2 * P * (t + 1)].bitcast(FP4X4),
                ws[:, H * z + P * t : H * z + P * (t + 1)],
                operand[0].bitcast(FP8X4),
                operand[1],
                start=(z == 0),
                stop=(z == 1),
            )

        def product(z_bf, bank_tag):
            operands = quantise(z_bf, 2)
            acc = pair.tile([P, PACK, BLK], F32, name="acc", tag=bank_tag)
            for t in range(PACK):
                for z in range(2):
                    one_pass(acc[:, t, :], t, z, operands[z])
            return acc

        def planes(b, o32, acc=None):
            cols = slice(BLK * b, BLK * (b + 1))
            o_bf = work.tile([P, BLK * PACK], BF16, name="o_bf", align_bytes=64)
            if acc is None:
                nc.vector.tensor_copy(o_bf[:].rearrange("p (j t) -> p j t", t=PACK), o32[:].rearrange("p t j -> p j t"))
            else:
                nc.scalar.copy(o_bf[:].rearrange("p (j t) -> p j t", t=PACK), acc[:].rearrange("p t j -> p j t"))
            nc.vector.quantize_mx(oc[:, cols].bitcast(FP8X4), os_[:, cols], o_bf[:])
            if b % 2 == 1:
                both = slice(BLK * (b - 1), BLK * (b + 1))
                nc.sync.dma_start(out1_v[:, both], oc[:, both].bitcast(I32))

        def hand_out(b, acc):
            o32 = work.tile([P, PACK, BLK], F32, name="o32", align_bytes=64)
            nc.scalar.copy(o32[:], acc[:])
            nc.sync.dma_start(out0_v[:, :, BLK * b : BLK * (b + 1)], o32[:])
            return o32

        banks = look_up([0, 1], ["ga", "gb", "gc", "gd"], ("B4", "B5", "B6", "B0"))
        z_bf = {0: mix_in_psum(0, banks[0], ("B7", "B1"))}
        banks.update(look_up([2, 3], ["gc", None, None, None], ("B4", "B5", "B7", "B1")))
        zT1 = [mix(1, z, banks[1]) for z in range(2)]
        zT2 = [mix(2, z, banks[2]) for z in range(2)]
        z_bf[1] = turn_back(zT1, "B3")
        acc = {0: product(z_bf[0], "B2")}
        zT3 = [mix(3, z, banks[3]) for z in range(2)]
        acc[1] = product(z_bf[1], "B6")
        z_bf[2] = turn_back(zT2, "B0")
        acc[2] = product(z_bf[2], "B4")
        last = [pair.tile([P, BLK], F32, name="last", tag=tag) for tag in ("B5", "B7", "B1", "B2")]
        operands, result = [], {}
        for z in range(2):
            operands.append(quantise(turn_back([zT3[z]], ("B3", "B0")[z]), 1)[0])
            if z == 0:
                result[0] = hand_out(0, acc[0])
            for t in range(PACK):
                one_pass(last[t][:], t, z, operands[z])
        for b in (1, 2):
            result[b] = hand_out(b, acc[b])
        planes(0, result[0])
        planes(1, result[1])
        o32 = work.tile([P, PACK, BLK], F32, name="o32", align_bytes=64)
        for t in range(PACK):
            if t % 2 == 0:
                nc.scalar.copy(o32[:, t, :], last[t][:])
            else:
                nc.vector.tensor_copy(o32[:, t, :], last[t][:])
        nc.sync.dma_start(out0_v[:, :, BLK * 3 : BLK * 4], o32[:])
        planes(2, result[2])
        planes(3, o32)
        for q in range(4):
            (nc.scalar, nc.sync)[q % 2].dma_start(out_2[0][4 * q : 4 * q + 4, :].bitcast(I32), os_[32 * q : 32 * q + 4, :].bitcast(I32))
